import numpy as np
import ml_dtypes


def mxq(x, axis, fmt="e4m3"):
    dtype, down = {"e4m3": (ml_dtypes.float8_e4m3fn, 7), "e5m2": (ml_dtypes.float8_e5m2, 14)}[fmt]
    v = np.moveaxis(np.asarray(x, np.float32).astype(ml_dtypes.bfloat16).astype(np.float64), axis, -1)
    blocks = v.reshape(v.shape[:-1] + (-1, 32))
    amax = np.abs(blocks).max(-1, keepdims=True)
    byte = np.maximum(np.where(amax > 0, np.frexp(amax)[1] - 1 + 127, 0) - down, 1)
    scale = np.exp2(byte - 127.0)
    codes = (blocks / scale).astype(np.float32).astype(dtype).astype(np.float64)
    return np.moveaxis((codes * scale).reshape(v.shape), -1, axis)


WIDE = False


def mx_kscale(k):
    if not WIDE:
        return np.ones(k)
    levels = np.array([10, -10, 5, -5, 0])
    if k % 512:
        return np.exp2(np.random.permutation(np.resize(levels, k // 32))).repeat(32)
    a = np.empty((k // 512, 16))
    for p in range(k // 512):
        a[p, :8] = np.random.permutation(np.resize(levels, 8))
        for g in range(8):
            far = levels[np.abs(levels - a[p, g]) >= 10]
            a[p, g + 8] = far[np.random.randint(len(far))]
    return np.exp2(a.ravel()).repeat(32)


def f64(x):
    return np.asarray(x).astype(np.float64)


def striped(idx):
    return np.tile(idx.reshape(-1, 16).T, (8, 1)).astype(np.uint16)


def unstriped(offs):
    return offs[:16].T.reshape(-1).astype(np.int64)


E2M1 = np.array([0.0, 0.5, 1.0, 1.5, 2.0, 3.0, 4.0, 6.0, -0.0, -0.5, -1.0, -1.5, -2.0, -3.0, -4.0, -6.0])


def pack_weight(w, fmt):
    k, n = w.shape
    w = f64(np.asarray(w, np.float32).astype(ml_dtypes.bfloat16)).reshape(k // 32, 32, n)
    amax = np.abs(w).max(1)
    if fmt == "e4m3":
        byte = np.frexp(amax)[1] - 1 + 127 - 7
    else:
        mant, ex = np.frexp(amax / 6.0)
        byte = np.where(mant > 0.5, ex, ex - 1) + 127
    byte = np.clip(np.where(amax > 0, byte, 1), 1, 254)
    scaled = (w * np.exp2(127.0 - byte)[:, None, :]).reshape(k, n).astype(np.float32)
    by_word = np.ascontiguousarray(scaled.reshape(k // 512, 128, 4, n).transpose(0, 1, 3, 2))
    if fmt == "e4m3":
        words = by_word.astype(ml_dtypes.float8_e4m3fn).view(np.uint8)
    else:
        c = by_word.astype(ml_dtypes.float4_e2m1fn).view(np.uint8) & 0xF
        words = (c[..., 0::2] | (c[..., 1::2] << 4)).reshape(k // 512, 128, 2 * n)
    return np.ascontiguousarray(words), np.ascontiguousarray(byte.astype(np.uint8).reshape(k // 512, 16, n))


def unpack_weight(words, scales, fmt):
    g, _, n = scales.shape
    words = np.ascontiguousarray(words).reshape(g, 128, n, -1)
    if fmt == "e4m3":
        vals = words.view(ml_dtypes.float8_e4m3fn).astype(np.float64)
    else:
        nib = np.empty((g, 128, n, 4), np.uint8)
        nib[..., 0::2] = words & 0xF
        nib[..., 1::2] = words >> 4
        vals = E2M1[nib]
    vals = vals * np.repeat(np.exp2(scales.astype(np.float64) - 127.0), 8, axis=1)[..., None]
    return vals.transpose(0, 1, 3, 2).reshape(g * 512, n)


def gelu(v):
    return 0.5 * v * (1.0 + np.tanh(np.sqrt(2.0 / np.pi) * (v + 0.044715 * v**3)))


K, T, S, H, T3, S2, T2, P = 1536, 2048, 512, 1024, 2048, 512, 1024, 512

def setup_inputs():
    n = np.random.standard_normal
    s = mx_kscale(K)[:, None]
    u = mx_kscale(H)[:, None]
    tab_words, tab_scales = pack_weight(n((K, T)) * s, "e4m3")
    tab2_words, tab2_scales = pack_weight(n((H, T3)) / u / np.sqrt(H), "e4m3")
    w4_words, w4_scales = pack_weight(0.7 * n((K, H)) / s * u.T / np.sqrt(K), "e2m1")
    return {
        "tab_words": tab_words, "tab_scales": tab_scales,
        "offs": striped(np.random.permutation(T)[:S]),
        "w1": (2.5 * n((K, H)) / s / np.sqrt(K)).astype(np.float32),
        "catch": (n((H, S)) * u).astype(np.float32),
        "w4_words": w4_words, "w4_scales": w4_scales,
        "page0": (n((H, T2)) * u).astype(np.float32),
        "wgs": np.exp(0.3 * n((128, S))).astype(np.float32),
        "offs3": striped(np.random.permutation(T2)[:S]),
        "gain": np.random.uniform(-0.5, 0.6, H).astype(np.float32),
        "tab2_words": tab2_words, "tab2_scales": tab2_scales,
        "offs2": striped(np.random.permutation(T3)[:S2]),
        "pos1": striped(np.random.permutation(T2)[:P]),
        "pos2": striped(np.random.permutation(T2)[:P]),
        "dep": np.exp(0.5 * n(S2)).astype(np.float32),
    }

def reference(tab_words, tab_scales, offs, w1, catch, w4_words, w4_scales, page0, wgs, offs3, gain, tab2_words, tab2_scales, offs2, pos1, pos2, dep):
    v = unpack_weight(tab_words, tab_scales, "e4m3")[:, unstriped(offs)]
    v2 = unpack_weight(tab2_words, tab2_scales, "e4m3")[:, unstriped(offs2)]
    w4 = unpack_weight(w4_words, w4_scales, "e2m1")
    a = mxq(f64(w1), 0, "e4m3").T @ v
    b = w4.T @ v
    h = np.log(1.0 + np.abs(a)) * f64(catch) + b
    page = f64(page0).copy()
    page[:, unstriped(offs3)] = np.tile(f64(wgs), (H // 128, 1)) * h
    x = mxq(np.maximum(page, f64(gain)[:, None] * page), 0, "e4m3")
    e = v2.T @ x
    out = e[:, unstriped(pos1)] * e[:, unstriped(pos2)] * f64(dep)[:, None]
    return out

@@ -1,0 +1,312 @@
+from contextlib import ExitStack
+
+import concourse.mybir as mybir
+
+K, T, S, H, T3, S2, T2, NP = 1536, 2048, 512, 1024, 2048, 512, 1024, 512
+FLOPS = 2 * (2 * K * H * S + H * S2 * T2)
+
+F32 = mybir.dt.float32
+BF16 = mybir.dt.bfloat16
+U32 = mybir.dt.uint32
+I32 = mybir.dt.int32
+U16 = mybir.dt.uint16
+U8 = mybir.dt.uint8
+FP8X4 = mybir.dt.float8_e4m3fn_x4
+FP4X4 = mybir.dt.float4_e2m1fn_x4
+ACT = mybir.ActivationFunctionType
+ALU = mybir.AluOpType
+
+P = 128
+PACK = 4
+KP = P * PACK
+PASS1 = K // KP
+PASS2 = H // KP
+TILES = H // P
+BANK = 512
+W1_BLOCKS = ((0, 1), (1, 2), (2, 3), (3, 4), (4, 6), (6, 8))
+W4_BLOCKS = ((0, 2), (2, 4), (4, 8))
+XCH = 256
+
+
+def tile_list_sediment_anomaly_scores_kernel(
+    tc, tab_words, tab_scales, offs, w1, catch, w4_words, w4_scales, page0, wgs, offs3, gain,
+    tab2_words, tab2_scales, offs2, pos1, pos2, dep, out,
+):
+    nc = tc.nc
+    with ExitStack() as ctx:
+        lists = ctx.enter_context(tc.tile_pool(name="lists", bufs=1))
+        keep = ctx.enter_context(tc.tile_pool(name="keep", bufs=1))
+        ring = ctx.enter_context(tc.tile_pool(name="ring", bufs=3))
+        psum = ctx.enter_context(tc.psum_pool(name="psum", bufs=4))
+
+        def load_list(name, src):
+            tile = lists.tile([P, src.shape[1]], U16, name=name)
+            nc.sync.dma_start(tile[:], src)
+            return tile
+
+        def load_words(name, src):
+            tile = keep.tile([P, src.shape[1]], U32, name=name, align_bytes=64)
+            nc.sync.dma_start(out=tile[:].bitcast(I32), in_=src.rearrange("p t i -> p (t i)").bitcast(I32))
+            return tile
+
+        def load_planes(queue, tile, src):
+            for q in range(4):
+                queue.dma_start(
+                    out=tile[32 * q : 32 * q + 4].bitcast(I32),
+                    in_=src[:, 4 * q : 4 * q + 4, :].rearrange("a r t -> r a t").bitcast(I32),
+                )
+
+        tab_planes = keep.tile([P, PASS1, T], U8, align_bytes=64)
+        w4_planes = keep.tile([P, PASS1, H], U8, align_bytes=64)
+        tab2_planes = keep.tile([P, T3], U8, align_bytes=64)
+        nc.vector.memset(tab_planes[:].bitcast(I32), 0)
+        nc.gpsimd.memset(w4_planes[:].bitcast(I32), 0)
+        nc.gpsimd.memset(tab2_planes[:].bitcast(I32), 0)
+
+        w1_raw = {}
+
+        def load_w1(block):
+            c0, c1 = block
+            width = (c1 - c0) * P
+            for a in range(PASS1):
+                if width == P:
+                    raw = keep.tile([P, PACK, width], F32, name="narrow", tag="narrow", bufs=12, align_bytes=64)
+                else:
+                    raw = keep.tile([P, PACK, width], F32, name="wide", tag="wide", bufs=6, align_bytes=64)
+                rows = w1[a * KP : (a + 1) * KP, c0 * P : c1 * P]
+                nc.sync.dma_start(out=raw[:], in_=rows.rearrange("(p j) c -> p j c", j=PACK))
+                for c in range(c0, c1):
+                    w1_raw[a, c] = raw[:, :, (c - c0) * P : (c - c0 + 1) * P]
+
+        w4_codes = {}
+
+        def load_w4(block):
+            c0, c1 = block
+            tile = keep.tile([P, PASS1, (c1 - c0) * 2 * P], U8, name=f"w4_{c0}", align_bytes=64)
+            nc.sync.dma_start(
+                out=tile[:].bitcast(I32),
+                in_=w4_words[:, :, c0 * 2 * P : c1 * 2 * P].rearrange("a p c -> p a c").bitcast(I32),
+            )
+            for a in range(PASS1):
+                for c in range(c0, c1):
+                    w4_codes[a, c] = tile[:, a, (c - c0) * 2 * P : (c - c0 + 1) * 2 * P]
+
+        catch_sb, pages = {}, {}
+
+        def load_catch(c):
+            catch_sb[c] = keep.tile([P, S], F32, name="row512", tag="row512", bufs=8)
+            nc.sync.dma_start(out=catch_sb[c][:], in_=catch[c * P : (c + 1) * P, :])
+
+        def load_page(c):
+            pages[c] = keep.tile([P, T2], F32, name=f"page{c}", tag=f"page{c}", align_bytes=64)
+            nc.sync.dma_start(out=pages[c][:], in_=page0[c * P : (c + 1) * P, :])
+
+        idx = load_list("idx", offs)
+        tab = [load_words("tab0", tab_words[0])]
+        load_planes(nc.sync, tab_planes, tab_scales)
+        load_planes(nc.gpsimd, w4_planes, w4_scales)
+        tab.append(load_words("tab1", tab_words[1]))
+        load_w1(W1_BLOCKS[0])
+        tab.append(load_words("tab2", tab_words[2]))
+        load_w4(W4_BLOCKS[0])
+        load_catch(0)
+        wgs_sb = keep.tile([P, S], F32)
+        nc.sync.dma_start(out=wgs_sb[:], in_=wgs)
+        idx3 = load_list("idx3", offs3)
+        load_page(0)
+        load_w1(W1_BLOCKS[1])
+        load_catch(1)
+        gain_sb = keep.tile([P, TILES], F32)
+        with nc.allow_non_contiguous_dma(reason="one gain a partition"):
+            nc.sync.dma_start(out=gain_sb[:], in_=gain.rearrange("(c p) -> p c", p=P))
+        load_w4(W4_BLOCKS[1])
+        load_w1(W1_BLOCKS[2])
+        load_catch(2)
+        load_page(1)
+        load_w1(W1_BLOCKS[3])
+        load_catch(3)
+        load_page(2)
+        load_w4(W4_BLOCKS[2])
+        load_w1(W1_BLOCKS[4])
+        load_catch(4)
+        load_page(3)
+        load_catch(5)
+        load_w1(W1_BLOCKS[5])
+        load_page(4)
+        load_catch(6)
+        load_catch(7)
+        for c in range(5, TILES):
+            load_page(c)
+        idx2 = load_list("idx2", offs2)
+        p1 = load_list("p1", pos1)
+        p2 = load_list("p2", pos2)
+        dep_sb = keep.tile([P, S2 // P], F32)
+        with nc.allow_non_contiguous_dma(reason="one weight a partition"):
+            nc.sync.dma_start(out=dep_sb[:], in_=dep.rearrange("(c p) -> p c", p=P))
+        for q in range(4):
+            nc.sync.dma_start(
+                out=tab2_planes[32 * q : 32 * q + 4 * PASS2, :].bitcast(I32),
+                in_=tab2_scales[:, 4 * q : 4 * q + 4, :].bitcast(I32),
+            )
+        tab2 = [load_words(f"tab2_{b}", tab2_words[b]) for b in range(PASS2)]
+
+        v_codes, v_planes = [], []
+        for a in range(PASS1):
+            plane = keep.tile([P, S], U8, name=f"v_plane{a}", align_bytes=64)
+            nc.vector.tensor_copy(plane[:], tab_planes[:, a, :].indirect(idx[:]))
+            v_planes.append(plane)
+        for a in range(PASS1):
+            codes = keep.tile([P, S], U32, name=f"v_codes{a}", align_bytes=64)
+            nc.vector.tensor_copy(codes[:], tab[a][:].indirect(idx[:]))
+            v_codes.append(codes)
+
+        b_banks, logs, feats, rounded = {}, {}, {}, {}
+
+        def first_stage(c):
+            grouped = ring.tile([P, PASS1, P, PACK], BF16, name="w1_grouped", align_bytes=64, bufs=2)
+            for a in range(PASS1):
+                nc.scalar.copy(
+                    out=grouped[:, a].rearrange("p (c i) t -> p c t i", i=4),
+                    in_=w1_raw[a, c].rearrange("p t (c i) -> p c t i", i=4),
+                )
+            codes = ring.tile([P, PASS1 * P], U32, name="w1_codes", align_bytes=64)
+            plane = ring.tile([P, PASS1 * P], U8, name="w1_plane", align_bytes=64)
+            nc.vector.quantize_mx(
+                out=codes[:].bitcast(FP8X4), scales=plane[:], in_=grouped[:].rearrange("p a c t -> p (a c t)")
+            )
+            a_bank = psum.tile([P, S], F32, name="ab", tag="ab")
+            b_banks[c] = psum.tile([P, S], F32, name="ab", tag="ab")
+            for a in range(PASS1):
+                nc.tensor.matmul_mx(
+                    out=a_bank[:], lhsT=codes[:, a * P : (a + 1) * P].bitcast(FP8X4),
+                    lhsT_scale=plane[:, a * P : (a + 1) * P],
+                    rhs=v_codes[a][:].bitcast(FP8X4), rhs_scale=v_planes[a][:],
+                    start=(a == 0), stop=(a == PASS1 - 1),
+                )
+            for a in range(PASS1):
+                nc.tensor.matmul_mx(
+                    out=b_banks[c][:], lhsT=w4_codes[a, c].bitcast(FP4X4),
+                    lhsT_scale=w4_planes[:, a, c * P : (c + 1) * P],
+                    rhs=v_codes[a][:].bitcast(FP8X4), rhs_scale=v_planes[a][:],
+                    start=(a == 0), stop=(a == PASS1 - 1),
+                )
+            logs[c] = ring.tile([P, S], F32, name="log", bufs=2)
+            nc.scalar.activation(logs[c][:], a_bank[:], ACT.Abs)
+            nc.scalar.activation(logs[c][:], logs[c][:], ACT.Ln, bias=1.0)
+
+        def times_catch(c):
+            feats[c] = ring.tile([P, S], F32, name="feat", bufs=2)
+            nc.vector.tensor_tensor(feats[c][:], logs[c][:], catch_sb[c][:], ALU.mult)
+
+        def plus_b(c):
+            nc.vector.tensor_tensor(feats[c][:], feats[c][:], b_banks[c][:], ALU.add)
+
+        def refresh(c):
+            nc.vector.tensor_tensor(pages[c][:].indirect(idx3[:]), feats[c][:], wgs_sb[:], ALU.mult)
+
+        def rectify(c):
+            rounded[c] = keep.tile([P, T2], BF16, name="narrow", tag="narrow", bufs=12, align_bytes=64)
+            nc.vector.scalar_tensor_tensor(
+                rounded[c][:], pages[c][:], gain_sb[:, c : c + 1], pages[c][:], ALU.mult, ALU.max
+            )
+
+        first_stage(0)
+        times_catch(0)
+        plus_b(0)
+        first_stage(1)
+        refresh(0)
+        times_catch(1)
+        first_stage(2)
+        plus_b(1)
+        for c in range(TILES):
+            if c > 0:
+                refresh(c)
+            if c + 2 < TILES:
+                times_catch(c + 2)
+            rectify(c)
+            if c + 2 < TILES:
+                plus_b(c + 2)
+            if c + 3 < TILES:
+                first_stage(c + 3)
+
+        dealt = [keep.tile([P, PACK, T2], BF16, name=f"dealt{b}") for b in range(PASS2)]
+        for c in range(TILES):
+            b, quarter = divmod(c, PACK)
+            for t in range(PACK):
+                nc.sync.dma_start(out=dealt[b][32 * quarter : 32 * quarter + 32, t, :], in_=rounded[c][t:P:PACK, :])
+
+        v2_plane = keep.tile([P, S2], U8, align_bytes=64)
+        nc.vector.tensor_copy(v2_plane[:], tab2_planes[:].indirect(idx2[:]))
+        v2_codes = keep.tile([P, PASS2, S2], U32, name="v2_codes", tag=f"page{TILES - 1}", align_bytes=64)
+        for b in range(PASS2):
+            nc.vector.tensor_copy(v2_codes[:, b, :], tab2[b][:].indirect(idx2[:]))
+
+        dep_rows = []
+        for i in range(S2 // P):
+            rows = keep.tile([P, NP], F32, name="row512", tag="row512", bufs=8)
+            nc.scalar.copy(out=rows[:], in_=dep_sb[:, i : i + 1].to_broadcast([P, NP]))
+            dep_rows.append(rows)
+
+        x_codes, x_planes = [], []
+        for b in range(PASS2):
+            x_codes.append(keep.tile([P, T2], U32, name=f"x_codes{b}", align_bytes=64))
+            x_planes.append(keep.tile([P, T2], U8, name=f"x_plane{b}", align_bytes=64))
+            groups = []
+            for n0 in range(0, T2, XCH):
+                grouped = ring.tile([P, XCH, PACK], BF16, name="x_grouped", align_bytes=64, bufs=4)
+                dst = grouped[:].rearrange("p (c i) t -> p c t i", i=4)
+                src = dealt[b][:, :, n0 : n0 + XCH].rearrange("p t (c i) -> p c t i", i=4)
+                if b == PASS2 - 1 and (n0 // XCH) % 2 == 1:
+                    nc.vector.tensor_copy(out=dst, in_=src)
+                else:
+                    nc.scalar.copy(out=dst, in_=src)
+                groups.append(grouped)
+            for n0, grouped in zip(range(0, T2, XCH), groups):
+                nc.vector.quantize_mx(
+                    out=x_codes[b][:, n0 : n0 + XCH].bitcast(FP8X4), scales=x_planes[b][:, n0 : n0 + XCH],
+                    in_=grouped[:].rearrange("p n t -> p (n t)"),
+                )
+
+        scores, e_banks = {}, {}
+
+        def second_stage(i, n0, b):
+            nc.tensor.matmul_mx(
+                out=e_banks[i, n0][:], lhsT=v2_codes[:, b, i * P : (i + 1) * P].bitcast(FP8X4),
+                lhsT_scale=v2_plane[4 * b : P, i * P : (i + 1) * P],
+                rhs=x_codes[b][:, n0 : n0 + BANK].bitcast(FP8X4), rhs_scale=x_planes[b][:, n0 : n0 + BANK],
+                start=(b == 0), stop=(b == PASS2 - 1),
+            )
+
+        for i in range(S2 // P):
+            for n0 in range(0, T2, BANK):
+                e_banks[i, n0] = psum.tile([P, BANK], F32, name="e", tag="e" if i < 2 else "ab")
+                second_stage(i, n0, 0)
+
+        def score(i):
+            scores[i] = keep.tile([P, T2], F32, name="wide", tag="wide", bufs=6, align_bytes=64)
+            for n0 in range(0, T2, BANK):
+                second_stage(i, n0, 1)
+                bank = e_banks[i, n0]
+                if i == 0 and n0 > 0:
+                    nc.vector.tensor_copy(out=scores[i][:, n0 : n0 + BANK], in_=bank[:])
+                else:
+                    nc.scalar.copy(out=scores[i][:, n0 : n0 + BANK], in_=bank[:])
+
+        firsts = {}
+
+        def pick_first(i):
+            firsts[i] = keep.tile([P, NP], F32, name="row512", tag="row512", bufs=8)
+            nc.vector.tensor_tensor(firsts[i][:], scores[i][:].indirect(p1[:]), dep_rows[i][:], ALU.mult)
+
+        def pick_second(i):
+            result = keep.tile([P, NP], F32, name="row512", tag="row512", bufs=8)
+            nc.vector.tensor_tensor(result[:], scores[i][:].indirect(p2[:]), firsts[i][:], ALU.mult)
+            nc.sync.dma_start(out=out[i * P : (i + 1) * P, :], in_=result[:])
+
+        for i in range(S2 // P):
+            score(i)
+        pick_first(0)
+        for i in range(S2 // P):
+            if i + 1 < S2 // P:
+                pick_first(i + 1)
+            pick_second(i)

@@ -1,6 +1,7 @@
 from contextlib import ExitStack
 
 import concourse.mybir as mybir
+from concourse.masks import make_identity
 
 K, T, S, H, T3, S2, T2, NP = 1536, 2048, 512, 1024, 2048, 512, 1024, 512
 FLOPS = 2 * (2 * K * H * S + H * S2 * T2)
@@ -25,7 +26,10 @@ TILES = H // P
 BANK = 512
 W1_BLOCKS = ((0, 1), (1, 2), (2, 3), (3, 4), (4, 6), (6, 8))
 W4_BLOCKS = ((0, 2), (2, 4), (4, 8))
+W4_PLANE_BLOCKS = ((0, 2), (2, 8))
 XCH = 256
+WHOLE = ((0, S),)
+HALVES = ((0, S // 2), (S // 2, S))
 
 
 def tile_list_sediment_anomaly_scores_kernel(
@@ -57,10 +61,22 @@ def tile_list_sediment_anomaly_scores_kernel(
                 )
 
         tab_planes = keep.tile([P, PASS1, T], U8, align_bytes=64)
-        w4_planes = keep.tile([P, PASS1, H], U8, align_bytes=64)
+        w4_planes = [
+            keep.tile([P, PASS1, (c1 - c0) * P], U8, name=f"w4_planes{c0}", align_bytes=64) for c0, c1 in W4_PLANE_BLOCKS
+        ]
+        vectors = keep.tile([P, P], F32)
+        identity = keep.tile([P, P], F32)
+        warm = keep.tile([P, 1], F32)
+        nc.gpsimd.memset(warm[:], 1.0)
+        nc.scalar.activation(warm[:], warm[:], ACT.Ln)
         tab2_planes = keep.tile([P, T3], U8, align_bytes=64)
         nc.vector.memset(tab_planes[:].bitcast(I32), 0)
-        nc.gpsimd.memset(w4_planes[:].bitcast(I32), 0)
+        nc.gpsimd.memset(w4_planes[0][:].bitcast(I32), 0)
+        nc.gpsimd.memset(vectors[:], 0.0)
+        load_planes(nc.gpsimd, w4_planes[0], w4_scales[:, :, : W4_PLANE_BLOCKS[0][1] * P])
+        make_identity(nc, identity[:])
+        nc.gpsimd.memset(w4_planes[1][:].bitcast(I32), 0)
+        load_planes(nc.gpsimd, w4_planes[1], w4_scales[:, :, W4_PLANE_BLOCKS[1][0] * P :])
         nc.gpsimd.memset(tab2_planes[:].bitcast(I32), 0)
 
         w1_raw = {}
@@ -104,7 +120,6 @@ def tile_list_sediment_anomaly_scores_kernel(
         idx = load_list("idx", offs)
         tab = [load_words("tab0", tab_words[0])]
         load_planes(nc.sync, tab_planes, tab_scales)
-        load_planes(nc.gpsimd, w4_planes, w4_scales)
         tab.append(load_words("tab1", tab_words[1]))
         load_w1(W1_BLOCKS[0])
         tab.append(load_words("tab2", tab_words[2]))
@@ -114,11 +129,10 @@ def tile_list_sediment_anomaly_scores_kernel(
         nc.sync.dma_start(out=wgs_sb[:], in_=wgs)
         idx3 = load_list("idx3", offs3)
         load_page(0)
+        nc.sync.dma_start(out=vectors[0:TILES, :], in_=gain.rearrange("(c p) -> c p", p=P))
+        nc.sync.dma_start(out=vectors[TILES : TILES + S2 // P, :], in_=dep.rearrange("(c p) -> c p", p=P))
         load_w1(W1_BLOCKS[1])
         load_catch(1)
-        gain_sb = keep.tile([P, TILES], F32)
-        with nc.allow_non_contiguous_dma(reason="one gain a partition"):
-            nc.sync.dma_start(out=gain_sb[:], in_=gain.rearrange("(c p) -> p c", p=P))
         load_w4(W4_BLOCKS[1])
         load_w1(W1_BLOCKS[2])
         load_catch(2)
@@ -140,9 +154,6 @@ def tile_list_sediment_anomaly_scores_kernel(
         idx2 = load_list("idx2", offs2)
         p1 = load_list("p1", pos1)
         p2 = load_list("p2", pos2)
-        dep_sb = keep.tile([P, S2 // P], F32)
-        with nc.allow_non_contiguous_dma(reason="one weight a partition"):
-            nc.sync.dma_start(out=dep_sb[:], in_=dep.rearrange("(c p) -> p c", p=P))
         for q in range(4):
             nc.sync.dma_start(
                 out=tab2_planes[32 * q : 32 * q + 4 * PASS2, :].bitcast(I32),
@@ -157,10 +168,19 @@ def tile_list_sediment_anomaly_scores_kernel(
             v_planes.append(plane)
         for a in range(PASS1):
             codes = keep.tile([P, S], U32, name=f"v_codes{a}", align_bytes=64)
-            nc.vector.tensor_copy(codes[:], tab[a][:].indirect(idx[:]))
+            for j0, j1 in (HALVES if a == PASS1 - 1 else WHOLE):
+                nc.vector.tensor_copy(codes[:, j0:j1], tab[a][:].indirect(idx[:, j0 // 16 : j1 // 16]))
             v_codes.append(codes)
 
+        turned = psum.tile([P, P], F32, name="e", tag="e")
+        nc.tensor.transpose(turned[:], vectors[:], identity[:])
+        columns = keep.tile([P, TILES + S2 // P], F32)
+        nc.scalar.copy(out=columns[:], in_=turned[:, : TILES + S2 // P])
+
         b_banks, logs, feats, rounded = {}, {}, {}, {}
+
+        def pieces(c):
+            return HALVES if c == 0 else WHOLE
 
         def first_stage(c):
             grouped = ring.tile([P, PASS1, P, PACK], BF16, name="w1_grouped", align_bytes=64, bufs=2)
@@ -174,47 +194,53 @@ def tile_list_sediment_anomaly_scores_kernel(
             nc.vector.quantize_mx(
                 out=codes[:].bitcast(FP8X4), scales=plane[:], in_=grouped[:].rearrange("p a c t -> p (a c t)")
             )
-            a_bank = psum.tile([P, S], F32, name="ab", tag="ab")
-            b_banks[c] = psum.tile([P, S], F32, name="ab", tag="ab")
-            for a in range(PASS1):
-                nc.tensor.matmul_mx(
-                    out=a_bank[:], lhsT=codes[:, a * P : (a + 1) * P].bitcast(FP8X4),
-                    lhsT_scale=plane[:, a * P : (a + 1) * P],
-                    rhs=v_codes[a][:].bitcast(FP8X4), rhs_scale=v_planes[a][:],
-                    start=(a == 0), stop=(a == PASS1 - 1),
-                )
-            for a in range(PASS1):
-                nc.tensor.matmul_mx(
-                    out=b_banks[c][:], lhsT=w4_codes[a, c].bitcast(FP4X4),
-                    lhsT_scale=w4_planes[:, a, c * P : (c + 1) * P],
-                    rhs=v_codes[a][:].bitcast(FP8X4), rhs_scale=v_planes[a][:],
-                    start=(a == 0), stop=(a == PASS1 - 1),
-                )
-            logs[c] = ring.tile([P, S], F32, name="log", bufs=2)
-            nc.scalar.activation(logs[c][:], a_bank[:], ACT.Abs)
-            nc.scalar.activation(logs[c][:], logs[c][:], ACT.Ln, bias=1.0)
+            c0 = max(b0 for b0, b1 in W4_PLANE_BLOCKS if b0 <= c)
+            w4_plane = w4_planes[0 if c0 == 0 else 1]
+            for j0, j1 in pieces(c):
+                tag = "e" if j0 > 0 else "ab"
+                a_bank = psum.tile([P, j1 - j0], F32, name="a_bank", tag=tag)
+                b_banks[c, j0] = psum.tile([P, j1 - j0], F32, name="b_bank", tag=tag)
+                for a in range(PASS1):
+                    nc.tensor.matmul_mx(
+                        out=a_bank[:], lhsT=codes[:, a * P : (a + 1) * P].bitcast(FP8X4),
+                        lhsT_scale=plane[:, a * P : (a + 1) * P],
+                        rhs=v_codes[a][:, j0:j1].bitcast(FP8X4), rhs_scale=v_planes[a][:, j0:j1],
+                        start=(a == 0), stop=(a == PASS1 - 1),
+                    )
+                for a in range(PASS1):
+                    nc.tensor.matmul_mx(
+                        out=b_banks[c, j0][:], lhsT=w4_codes[a, c].bitcast(FP4X4),
+                        lhsT_scale=w4_plane[:, a, (c - c0) * P : (c - c0 + 1) * P],
+                        rhs=v_codes[a][:, j0:j1].bitcast(FP8X4), rhs_scale=v_planes[a][:, j0:j1],
+                        start=(a == 0), stop=(a == PASS1 - 1),
+                    )
+                logs[c, j0] = ring.tile([P, j1 - j0], F32, name="log", bufs=3)
+                nc.scalar.activation(logs[c, j0][:], a_bank[:], ACT.Abs)
+                nc.scalar.activation(logs[c, j0][:], logs[c, j0][:], ACT.Ln, bias=1.0)
 
-        def times_catch(c):
-            feats[c] = ring.tile([P, S], F32, name="feat", bufs=2)
-            nc.vector.tensor_tensor(feats[c][:], logs[c][:], catch_sb[c][:], ALU.mult)
+        def times_catch(c, j0=0, j1=S):
+            feats[c, j0] = ring.tile([P, j1 - j0], F32, name="feat", bufs=2)
+            nc.vector.tensor_tensor(feats[c, j0][:], logs[c, j0][:], catch_sb[c][:, j0:j1], ALU.mult)
 
-        def plus_b(c):
-            nc.vector.tensor_tensor(feats[c][:], feats[c][:], b_banks[c][:], ALU.add)
+        def plus_b(c, j0=0):
+            nc.vector.tensor_tensor(feats[c, j0][:], feats[c, j0][:], b_banks[c, j0][:], ALU.add)
 
-        def refresh(c):
-            nc.vector.tensor_tensor(pages[c][:].indirect(idx3[:]), feats[c][:], wgs_sb[:], ALU.mult)
+        def refresh(c, j0=0, j1=S):
+            window = pages[c][:].indirect(idx3[:, j0 // 16 : j1 // 16])
+            nc.vector.tensor_tensor(window, feats[c, j0][:], wgs_sb[:, j0:j1], ALU.mult)
 
         def rectify(c):
             rounded[c] = keep.tile([P, T2], BF16, name="narrow", tag="narrow", bufs=12, align_bytes=64)
             nc.vector.scalar_tensor_tensor(
-                rounded[c][:], pages[c][:], gain_sb[:, c : c + 1], pages[c][:], ALU.mult, ALU.max
+                rounded[c][:], pages[c][:], columns[:, c : c + 1], pages[c][:], ALU.mult, ALU.max
             )
 
         first_stage(0)
-        times_catch(0)
-        plus_b(0)
+        for j0, j1 in HALVES:
+            times_catch(0, j0, j1)
+            plus_b(0, j0)
+            refresh(0, j0, j1)
         first_stage(1)
-        refresh(0)
         times_catch(1)
         first_stage(2)
         plus_b(1)
@@ -244,7 +270,7 @@ def tile_list_sediment_anomaly_scores_kernel(
         dep_rows = []
         for i in range(S2 // P):
             rows = keep.tile([P, NP], F32, name="row512", tag="row512", bufs=8)
-            nc.scalar.copy(out=rows[:], in_=dep_sb[:, i : i + 1].to_broadcast([P, NP]))
+            nc.scalar.copy(out=rows[:], in_=columns[:, TILES + i : TILES + i + 1].to_broadcast([P, NP]))
             dep_rows.append(rows)
 
         x_codes, x_planes = [], []

from contextlib import ExitStack

import concourse.mybir as mybir
from concourse.masks import make_identity

K, T, S, H, T3, S2, T2, NP = 1536, 2048, 512, 1024, 2048, 512, 1024, 512
FLOPS = 2 * (2 * K * H * S + H * S2 * T2)

F32 = mybir.dt.float32
BF16 = mybir.dt.bfloat16
U32 = mybir.dt.uint32
I32 = mybir.dt.int32
U16 = mybir.dt.uint16
U8 = mybir.dt.uint8
FP8X4 = mybir.dt.float8_e4m3fn_x4
FP4X4 = mybir.dt.float4_e2m1fn_x4
ACT = mybir.ActivationFunctionType
ALU = mybir.AluOpType

P = 128
PACK = 4
KP = P * PACK
PASS1 = K // KP
PASS2 = H // KP
TILES = H // P
BANK = 512
W1_BLOCKS = ((0, 1), (1, 2), (2, 3), (3, 4), (4, 6), (6, 8))
W4_BLOCKS = ((0, 2), (2, 4), (4, 8))
W4_PLANE_BLOCKS = ((0, 2), (2, 8))
XCH = 256
WHOLE = ((0, S),)
HALVES = ((0, S // 2), (S // 2, S))


def tile_list_sediment_anomaly_scores_kernel(
    tc, tab_words, tab_scales, offs, w1, catch, w4_words, w4_scales, page0, wgs, offs3, gain,
    tab2_words, tab2_scales, offs2, pos1, pos2, dep, out,
):
    nc = tc.nc
    with ExitStack() as ctx:
        lists = ctx.enter_context(tc.tile_pool(name="lists", bufs=1))
        keep = ctx.enter_context(tc.tile_pool(name="keep", bufs=1))
        ring = ctx.enter_context(tc.tile_pool(name="ring", bufs=3))
        psum = ctx.enter_context(tc.psum_pool(name="psum", bufs=4))

        def load_list(name, src):
            tile = lists.tile([P, src.shape[1]], U16, name=name)
            nc.sync.dma_start(tile[:], src)
            return tile

        def load_words(name, src):
            tile = keep.tile([P, src.shape[1]], U32, name=name, align_bytes=64)
            nc.sync.dma_start(out=tile[:].bitcast(I32), in_=src.rearrange("p t i -> p (t i)").bitcast(I32))
            return tile

        def load_planes(queue, tile, src):
            for q in range(4):
                queue.dma_start(
                    out=tile[32 * q : 32 * q + 4].bitcast(I32),
                    in_=src[:, 4 * q : 4 * q + 4, :].rearrange("a r t -> r a t").bitcast(I32),
                )

        tab_planes = keep.tile([P, PASS1, T], U8, align_bytes=64)
        w4_planes = [
            keep.tile([P, PASS1, (c1 - c0) * P], U8, name=f"w4_planes{c0}", align_bytes=64) for c0, c1 in W4_PLANE_BLOCKS
        ]
        vectors = keep.tile([P, P], F32)
        identity = keep.tile([P, P], F32)
        warm = keep.tile([P, 1], F32)
        nc.gpsimd.memset(warm[:], 1.0)
        nc.scalar.activation(warm[:], warm[:], ACT.Ln)
        tab2_planes = keep.tile([P, T3], U8, align_bytes=64)
        nc.vector.memset(tab_planes[:].bitcast(I32), 0)
        nc.gpsimd.memset(w4_planes[0][:].bitcast(I32), 0)
        nc.gpsimd.memset(vectors[:], 0.0)
        load_planes(nc.gpsimd, w4_planes[0], w4_scales[:, :, : W4_PLANE_BLOCKS[0][1] * P])
        make_identity(nc, identity[:])
        nc.gpsimd.memset(w4_planes[1][:].bitcast(I32), 0)
        load_planes(nc.gpsimd, w4_planes[1], w4_scales[:, :, W4_PLANE_BLOCKS[1][0] * P :])
        nc.gpsimd.memset(tab2_planes[:].bitcast(I32), 0)

        w1_raw = {}

        def load_w1(block):
            c0, c1 = block
            width = (c1 - c0) * P
            for a in range(PASS1):
                if width == P:
                    raw = keep.tile([P, PACK, width], F32, name="narrow", tag="narrow", bufs=12, align_bytes=64)
                else:
                    raw = keep.tile([P, PACK, width], F32, name="wide", tag="wide", bufs=6, align_bytes=64)
                rows = w1[a * KP : (a + 1) * KP, c0 * P : c1 * P]
                nc.sync.dma_start(out=raw[:], in_=rows.rearrange("(p j) c -> p j c", j=PACK))
                for c in range(c0, c1):
                    w1_raw[a, c] = raw[:, :, (c - c0) * P : (c - c0 + 1) * P]

        w4_codes = {}

        def load_w4(block):
            c0, c1 = block
            tile = keep.tile([P, PASS1, (c1 - c0) * 2 * P], U8, name=f"w4_{c0}", align_bytes=64)
            nc.sync.dma_start(
                out=tile[:].bitcast(I32),
                in_=w4_words[:, :, c0 * 2 * P : c1 * 2 * P].rearrange("a p c -> p a c").bitcast(I32),
            )
            for a in range(PASS1):
                for c in range(c0, c1):
                    w4_codes[a, c] = tile[:, a, (c - c0) * 2 * P : (c - c0 + 1) * 2 * P]

        catch_sb, pages = {}, {}

        def load_catch(c):
            catch_sb[c] = keep.tile([P, S], F32, name="row512", tag="row512", bufs=8)
            nc.sync.dma_start(out=catch_sb[c][:], in_=catch[c * P : (c + 1) * P, :])

        def load_page(c):
            pages[c] = keep.tile([P, T2], F32, name=f"page{c}", tag=f"page{c}", align_bytes=64)
            nc.sync.dma_start(out=pages[c][:], in_=page0[c * P : (c + 1) * P, :])

        idx = load_list("idx", offs)
        tab = [load_words("tab0", tab_words[0])]
        load_planes(nc.sync, tab_planes, tab_scales)
        tab.append(load_words("tab1", tab_words[1]))
        load_w1(W1_BLOCKS[0])
        tab.append(load_words("tab2", tab_words[2]))
        load_w4(W4_BLOCKS[0])
        load_catch(0)
        wgs_sb = keep.tile([P, S], F32)
        nc.sync.dma_start(out=wgs_sb[:], in_=wgs)
        idx3 = load_list("idx3", offs3)
        load_page(0)
        nc.sync.dma_start(out=vectors[0:TILES, :], in_=gain.rearrange("(c p) -> c p", p=P))
        nc.sync.dma_start(out=vectors[TILES : TILES + S2 // P, :], in_=dep.rearrange("(c p) -> c p", p=P))
        load_w1(W1_BLOCKS[1])
        load_catch(1)
        load_w4(W4_BLOCKS[1])
        load_w1(W1_BLOCKS[2])
        load_catch(2)
        load_page(1)
        load_w1(W1_BLOCKS[3])
        load_catch(3)
        load_page(2)
        load_w4(W4_BLOCKS[2])
        load_w1(W1_BLOCKS[4])
        load_catch(4)
        load_page(3)
        load_catch(5)
        load_w1(W1_BLOCKS[5])
        load_page(4)
        load_catch(6)
        load_catch(7)
        for c in range(5, TILES):
            load_page(c)
        idx2 = load_list("idx2", offs2)
        p1 = load_list("p1", pos1)
        p2 = load_list("p2", pos2)
        for q in range(4):
            nc.sync.dma_start(
                out=tab2_planes[32 * q : 32 * q + 4 * PASS2, :].bitcast(I32),
                in_=tab2_scales[:, 4 * q : 4 * q + 4, :].bitcast(I32),
            )
        tab2 = [load_words(f"tab2_{b}", tab2_words[b]) for b in range(PASS2)]

        v_codes, v_planes = [], []
        for a in range(PASS1):
            plane = keep.tile([P, S], U8, name=f"v_plane{a}", align_bytes=64)
            nc.vector.tensor_copy(plane[:], tab_planes[:, a, :].indirect(idx[:]))
            v_planes.append(plane)
        for a in range(PASS1):
            codes = keep.tile([P, S], U32, name=f"v_codes{a}", align_bytes=64)
            for j0, j1 in (HALVES if a == PASS1 - 1 else WHOLE):
                nc.vector.tensor_copy(codes[:, j0:j1], tab[a][:].indirect(idx[:, j0 // 16 : j1 // 16]))
            v_codes.append(codes)

        turned = psum.tile([P, P], F32, name="e", tag="e")
        nc.tensor.transpose(turned[:], vectors[:], identity[:])
        columns = keep.tile([P, TILES + S2 // P], F32)
        nc.scalar.copy(out=columns[:], in_=turned[:, : TILES + S2 // P])

        b_banks, logs, feats, rounded = {}, {}, {}, {}

        def pieces(c):
            return HALVES if c == 0 else WHOLE

        def first_stage(c):
            grouped = ring.tile([P, PASS1, P, PACK], BF16, name="w1_grouped", align_bytes=64, bufs=2)
            for a in range(PASS1):
                nc.scalar.copy(
                    out=grouped[:, a].rearrange("p (c i) t -> p c t i", i=4),
                    in_=w1_raw[a, c].rearrange("p t (c i) -> p c t i", i=4),
                )
            codes = ring.tile([P, PASS1 * P], U32, name="w1_codes", align_bytes=64)
            plane = ring.tile([P, PASS1 * P], U8, name="w1_plane", align_bytes=64)
            nc.vector.quantize_mx(
                out=codes[:].bitcast(FP8X4), scales=plane[:], in_=grouped[:].rearrange("p a c t -> p (a c t)")
            )
            c0 = max(b0 for b0, b1 in W4_PLANE_BLOCKS if b0 <= c)
            w4_plane = w4_planes[0 if c0 == 0 else 1]
            for j0, j1 in pieces(c):
                tag = "e" if j0 > 0 else "ab"
                a_bank = psum.tile([P, j1 - j0], F32, name="a_bank", tag=tag)
                b_banks[c, j0] = psum.tile([P, j1 - j0], F32, name="b_bank", tag=tag)
                for a in range(PASS1):
                    nc.tensor.matmul_mx(
                        out=a_bank[:], lhsT=codes[:, a * P : (a + 1) * P].bitcast(FP8X4),
                        lhsT_scale=plane[:, a * P : (a + 1) * P],
                        rhs=v_codes[a][:, j0:j1].bitcast(FP8X4), rhs_scale=v_planes[a][:, j0:j1],
                        start=(a == 0), stop=(a == PASS1 - 1),
                    )
                for a in range(PASS1):
                    nc.tensor.matmul_mx(
                        out=b_banks[c, j0][:], lhsT=w4_codes[a, c].bitcast(FP4X4),
                        lhsT_scale=w4_plane[:, a, (c - c0) * P : (c - c0 + 1) * P],
                        rhs=v_codes[a][:, j0:j1].bitcast(FP8X4), rhs_scale=v_planes[a][:, j0:j1],
                        start=(a == 0), stop=(a == PASS1 - 1),
                    )
                logs[c, j0] = ring.tile([P, j1 - j0], F32, name="log", bufs=3)
                nc.scalar.activation(logs[c, j0][:], a_bank[:], ACT.Abs)
                nc.scalar.activation(logs[c, j0][:], logs[c, j0][:], ACT.Ln, bias=1.0)

        def times_catch(c, j0=0, j1=S):
            feats[c, j0] = ring.tile([P, j1 - j0], F32, name="feat", bufs=2)
            nc.vector.tensor_tensor(feats[c, j0][:], logs[c, j0][:], catch_sb[c][:, j0:j1], ALU.mult)

        def plus_b(c, j0=0):
            nc.vector.tensor_tensor(feats[c, j0][:], feats[c, j0][:], b_banks[c, j0][:], ALU.add)

        def refresh(c, j0=0, j1=S):
            window = pages[c][:].indirect(idx3[:, j0 // 16 : j1 // 16])
            nc.vector.tensor_tensor(window, feats[c, j0][:], wgs_sb[:, j0:j1], ALU.mult)

        def rectify(c):
            rounded[c] = keep.tile([P, T2], BF16, name="narrow", tag="narrow", bufs=12, align_bytes=64)
            nc.vector.scalar_tensor_tensor(
                rounded[c][:], pages[c][:], columns[:, c : c + 1], pages[c][:], ALU.mult, ALU.max
            )

        first_stage(0)
        for j0, j1 in HALVES:
            times_catch(0, j0, j1)
            plus_b(0, j0)
            refresh(0, j0, j1)
        first_stage(1)
        times_catch(1)
        first_stage(2)
        plus_b(1)
        for c in range(TILES):
            if c > 0:
                refresh(c)
            if c + 2 < TILES:
                times_catch(c + 2)
            rectify(c)
            if c + 2 < TILES:
                plus_b(c + 2)
            if c + 3 < TILES:
                first_stage(c + 3)

        dealt = [keep.tile([P, PACK, T2], BF16, name=f"dealt{b}") for b in range(PASS2)]
        for c in range(TILES):
            b, quarter = divmod(c, PACK)
            for t in range(PACK):
                nc.sync.dma_start(out=dealt[b][32 * quarter : 32 * quarter + 32, t, :], in_=rounded[c][t:P:PACK, :])

        v2_plane = keep.tile([P, S2], U8, align_bytes=64)
        nc.vector.tensor_copy(v2_plane[:], tab2_planes[:].indirect(idx2[:]))
        v2_codes = keep.tile([P, PASS2, S2], U32, name="v2_codes", tag=f"page{TILES - 1}", align_bytes=64)
        for b in range(PASS2):
            nc.vector.tensor_copy(v2_codes[:, b, :], tab2[b][:].indirect(idx2[:]))

        dep_rows = []
        for i in range(S2 // P):
            rows = keep.tile([P, NP], F32, name="row512", tag="row512", bufs=8)
            nc.scalar.copy(out=rows[:], in_=columns[:, TILES + i : TILES + i + 1].to_broadcast([P, NP]))
            dep_rows.append(rows)

        x_codes, x_planes = [], []
        for b in range(PASS2):
            x_codes.append(keep.tile([P, T2], U32, name=f"x_codes{b}", align_bytes=64))
            x_planes.append(keep.tile([P, T2], U8, name=f"x_plane{b}", align_bytes=64))
            groups = []
            for n0 in range(0, T2, XCH):
                grouped = ring.tile([P, XCH, PACK], BF16, name="x_grouped", align_bytes=64, bufs=4)
                dst = grouped[:].rearrange("p (c i) t -> p c t i", i=4)
                src = dealt[b][:, :, n0 : n0 + XCH].rearrange("p t (c i) -> p c t i", i=4)
                if b == PASS2 - 1 and (n0 // XCH) % 2 == 1:
                    nc.vector.tensor_copy(out=dst, in_=src)
                else:
                    nc.scalar.copy(out=dst, in_=src)
                groups.append(grouped)
            for n0, grouped in zip(range(0, T2, XCH), groups):
                nc.vector.quantize_mx(
                    out=x_codes[b][:, n0 : n0 + XCH].bitcast(FP8X4), scales=x_planes[b][:, n0 : n0 + XCH],
                    in_=grouped[:].rearrange("p n t -> p (n t)"),
                )

        scores, e_banks = {}, {}

        def second_stage(i, n0, b):
            nc.tensor.matmul_mx(
                out=e_banks[i, n0][:], lhsT=v2_codes[:, b, i * P : (i + 1) * P].bitcast(FP8X4),
                lhsT_scale=v2_plane[4 * b : P, i * P : (i + 1) * P],
                rhs=x_codes[b][:, n0 : n0 + BANK].bitcast(FP8X4), rhs_scale=x_planes[b][:, n0 : n0 + BANK],
                start=(b == 0), stop=(b == PASS2 - 1),
            )

        for i in range(S2 // P):
            for n0 in range(0, T2, BANK):
                e_banks[i, n0] = psum.tile([P, BANK], F32, name="e", tag="e" if i < 2 else "ab")
                second_stage(i, n0, 0)

        def score(i):
            scores[i] = keep.tile([P, T2], F32, name="wide", tag="wide", bufs=6, align_bytes=64)
            for n0 in range(0, T2, BANK):
                second_stage(i, n0, 1)
                bank = e_banks[i, n0]
                if i == 0 and n0 > 0:
                    nc.vector.tensor_copy(out=scores[i][:, n0 : n0 + BANK], in_=bank[:])
                else:
                    nc.scalar.copy(out=scores[i][:, n0 : n0 + BANK], in_=bank[:])

        firsts = {}

        def pick_first(i):
            firsts[i] = keep.tile([P, NP], F32, name="row512", tag="row512", bufs=8)
            nc.vector.tensor_tensor(firsts[i][:], scores[i][:].indirect(p1[:]), dep_rows[i][:], ALU.mult)

        def pick_second(i):
            result = keep.tile([P, NP], F32, name="row512", tag="row512", bufs=8)
            nc.vector.tensor_tensor(result[:], scores[i][:].indirect(p2[:]), firsts[i][:], ALU.mult)
            nc.sync.dma_start(out=out[i * P : (i + 1) * P, :], in_=result[:])

        for i in range(S2 // P):
            score(i)
        pick_first(0)
        for i in range(S2 // P):
            if i + 1 < S2 // P:
                pick_first(i + 1)
            pick_second(i)
